import numpy as np
import ml_dtypes


def mxq(x, axis, fmt="e4m3"):
    dtype, down = {"e4m3": (ml_dtypes.float8_e4m3fn, 7), "e5m2": (ml_dtypes.float8_e5m2, 14)}[fmt]
    v = np.moveaxis(np.asarray(x, np.float32).astype(ml_dtypes.bfloat16).astype(np.float64), axis, -1)
    blocks = v.reshape(v.shape[:-1] + (-1, 32))
    amax = np.abs(blocks).max(-1, keepdims=True)
    byte = np.maximum(np.where(amax > 0, np.frexp(amax)[1] - 1 + 127, 0) - down, 1)
    scale = np.exp2(byte - 127.0)
    codes = (blocks / scale).astype(np.float32).astype(dtype).astype(np.float64)
    return np.moveaxis((codes * scale).reshape(v.shape), -1, axis)


WIDE = False


def mx_kscale(k):
    if not WIDE:
        return np.ones(k)
    levels = np.array([10, -10, 5, -5, 0])
    if k % 512:
        return np.exp2(np.random.permutation(np.resize(levels, k // 32))).repeat(32)
    a = np.empty((k // 512, 16))
    for p in range(k // 512):
        a[p, :8] = np.random.permutation(np.resize(levels, 8))
        for g in range(8):
            far = levels[np.abs(levels - a[p, g]) >= 10]
            a[p, g + 8] = far[np.random.randint(len(far))]
    return np.exp2(a.ravel()).repeat(32)


def f64(x):
    return np.asarray(x).astype(np.float64)


def striped(idx):
    return np.tile(idx.reshape(-1, 16).T, (8, 1)).astype(np.uint16)


def unstriped(offs):
    return offs[:16].T.reshape(-1).astype(np.int64)


E2M1 = np.array([0.0, 0.5, 1.0, 1.5, 2.0, 3.0, 4.0, 6.0, -0.0, -0.5, -1.0, -1.5, -2.0, -3.0, -4.0, -6.0])


def pack_weight(w, fmt):
    k, n = w.shape
    w = f64(np.asarray(w, np.float32).astype(ml_dtypes.bfloat16)).reshape(k // 32, 32, n)
    amax = np.abs(w).max(1)
    if fmt == "e4m3":
        byte = np.frexp(amax)[1] - 1 + 127 - 7
    else:
        mant, ex = np.frexp(amax / 6.0)
        byte = np.where(mant > 0.5, ex, ex - 1) + 127
    byte = np.clip(np.where(amax > 0, byte, 1), 1, 254)
    scaled = (w * np.exp2(127.0 - byte)[:, None, :]).reshape(k, n).astype(np.float32)
    by_word = np.ascontiguousarray(scaled.reshape(k // 512, 128, 4, n).transpose(0, 1, 3, 2))
    if fmt == "e4m3":
        words = by_word.astype(ml_dtypes.float8_e4m3fn).view(np.uint8)
    else:
        c = by_word.astype(ml_dtypes.float4_e2m1fn).view(np.uint8) & 0xF
        words = (c[..., 0::2] | (c[..., 1::2] << 4)).reshape(k // 512, 128, 2 * n)
    return np.ascontiguousarray(words), np.ascontiguousarray(byte.astype(np.uint8).reshape(k // 512, 16, n))


def unpack_weight(words, scales, fmt):
    g, _, n = scales.shape
    words = np.ascontiguousarray(words).reshape(g, 128, n, -1)
    if fmt == "e4m3":
        vals = words.view(ml_dtypes.float8_e4m3fn).astype(np.float64)
    else:
        nib = np.empty((g, 128, n, 4), np.uint8)
        nib[..., 0::2] = words & 0xF
        nib[..., 1::2] = words >> 4
        vals = E2M1[nib]
    vals = vals * np.repeat(np.exp2(scales.astype(np.float64) - 127.0), 8, axis=1)[..., None]
    return vals.transpose(0, 1, 3, 2).reshape(g * 512, n)


def gelu(v):
    return 0.5 * v * (1.0 + np.tanh(np.sqrt(2.0 / np.pi) * (v + 0.044715 * v**3)))


K, T, S, H, T2, N = 1024, 2048, 512, 1024, 1024, 512

def setup_inputs():
    n = np.random.standard_normal
    s = mx_kscale(K)[:, None]
    u = mx_kscale(H)[:, None]
    w = mx_kscale(T2)[:, None]
    tab_words, tab_scales = pack_weight(n((K, T)) * s, "e4m3")
    wd_words, wd_scales = pack_weight(n((K, H)) / np.sqrt(K) / s, "e2m1")
    wl_words, wl_scales = pack_weight(n((H, N)) / np.sqrt(H) / u, "e4m3")
    return {
        "tab_words": tab_words, "tab_scales": tab_scales,
        "offs": striped(np.random.permutation(T)[:S]),
        "offs2": striped(np.random.permutation(T2)[:S]),
        "offs3": striped(np.random.permutation(T2)[:S]),
        "wd_words": wd_words, "wd_scales": wd_scales,
        "wr": (n((K, H)) / np.sqrt(K) / s * u.T).astype(np.float32),
        "wg1": np.exp(0.3 * n((128, S))).astype(np.float32),
        "wg2": np.exp(0.3 * n((128, S))).astype(np.float32),
        "fit": (0.4 * n((H, T2)) * u).astype(np.float32),
        "wl_words": wl_words, "wl_scales": wl_scales,
        "gs": (np.exp(0.3 * n(T2)) * w[:, 0]).astype(np.float32),
        "rm": (n((T2, T2)) / np.sqrt(T2) / w).astype(np.float32),
    }

def reference(tab_words, tab_scales, offs, offs2, offs3, wd_words, wd_scales, wr, wg1, wg2, fit, wl_words, wl_scales, gs, rm):
    v = unpack_weight(tab_words, tab_scales, "e4m3")[:, unstriped(offs)]
    d = unpack_weight(wd_words, wd_scales, "e2m1").T @ v
    h1 = d / (1.0 + np.exp(-d))
    h2 = mxq(f64(wr), 0, "e4m3").T @ v
    pageA = np.zeros((H, T2))
    pageA[:, unstriped(offs2)] = np.tile(f64(wg1), (H // 128, 1)) * h1
    pageB = np.zeros((H, T2))
    pageB[:, unstriped(offs3)] = np.tile(f64(wg2), (H // 128, 1)) * h2
    z = pageA * pageB + f64(fit)
    wl = unpack_weight(wl_words, wl_scales, "e4m3")
    e = (mxq(z, 0, "e4m3").T @ wl) * f64(gs)[:, None]
    return mxq(e, 0, "e4m3").T @ mxq(f64(rm), 0, "e4m3")

@@ -1,0 +1,288 @@
+from contextlib import ExitStack
+
+import concourse.mybir as mybir
+from concourse.masks import make_identity
+
+K, T, S, H, T2, N = 1024, 2048, 512, 1024, 1024, 512
+FLOPS = 2 * (2 * K * H * S + H * T2 * N + T2 * N * T2)
+
+F32 = mybir.dt.float32
+BF16 = mybir.dt.bfloat16
+I32 = mybir.dt.int32
+U32 = mybir.dt.uint32
+U16 = mybir.dt.uint16
+U8 = mybir.dt.uint8
+FP8X4 = mybir.dt.float8_e4m3fn_x4
+FP4X4 = mybir.dt.float4_e2m1fn_x4
+MULT = mybir.AluOpType.mult
+SILU = mybir.ActivationFunctionType.Silu
+
+P = 128
+BANK = 512
+PAGES_A = 3
+PAGES_B = 1
+
+
+def tile_list_donor_slot_mixing_kernel(
+    tc, tab_words, tab_scales, offs, offs2, offs3, wd_words, wd_scales, wr, wg1, wg2, fit, wl_words, wl_scales, gs, rm, out
+):
+    nc = tc.nc
+    with ExitStack() as ctx:
+        lists = ctx.enter_context(tc.tile_pool(name="lists", bufs=1))
+        keep = ctx.enter_context(tc.tile_pool(name="keep", bufs=1))
+        ring = ctx.enter_context(tc.tile_pool(name="ring", bufs=2))
+        psum = ctx.enter_context(tc.psum_pool(name="psum", bufs=1))
+
+        def held(shape, dtype, name, tag=None):
+            return keep.tile(shape, dtype, name=name, tag=tag or name, align_bytes=64)
+
+        def bank(i):
+            return psum.tile([P, BANK], F32, name="bank%d" % i, tag="bank%d" % i)
+
+        def load_list(src, name):
+            t = lists.tile([P, S // 16], U16, name=name)
+            nc.sync.dma_start(t[:], src)
+            return t
+
+        def scale_plane(width, name):
+            plane = held([P, 2 * width], U8, name)
+            nc.vector.memset(plane[:].bitcast(I32), 0)
+            return plane
+
+        def load_scales(queue, plane, src):
+            rows = src.rearrange("a (q r) c -> r q a c", r=4)
+            for r in range(4):
+                queue.dma_start(
+                    out=plane[r:P:32, :].bitcast(I32).rearrange("q (a c) -> q a c", a=2),
+                    in_=rows[r].bitcast(I32),
+                )
+
+        def mx(acc, lhs, lhs_s, rhs, rhs_s, start, stop, lhs_dt=FP8X4):
+            nc.tensor.matmul_mx(
+                out=acc, lhsT=lhs.bitcast(lhs_dt), lhsT_scale=lhs_s, rhs=rhs.bitcast(FP8X4), rhs_scale=rhs_s,
+                start=start, stop=stop,
+            )
+
+        tab_s = scale_plane(T, "tab_s")
+        wd_s = scale_plane(H, "wd_s")
+        idx = load_list(offs, "idx")
+        tab_w = [held([P, T], U32, "tab_w%d" % a) for a in range(2)]
+
+        def load_tab(a):
+            nc.sync.dma_start(out=tab_w[a][:].bitcast(I32), in_=tab_words[a].rearrange("p n i -> p (n i)").bitcast(I32))
+
+        load_tab(0)
+        load_scales(nc.sync, tab_s, tab_scales)
+        load_tab(1)
+        wd_w = held([P, 2, 2 * H], U8, "wd_w")
+        nc.sync.dma_start(out=wd_w[:].bitcast(I32), in_=wd_words.rearrange("a p n -> p a n").bitcast(I32))
+        load_scales(nc.sync, wd_s, wd_scales)
+        idx2 = load_list(offs2, "idx2")
+        wg1_sb = held([P, S], F32, "wg1_sb")
+        nc.sync.dma_start(out=wg1_sb[:], in_=wg1)
+
+        page_a = [held([P, T2], F32, "page_a%d" % i) for i in range(PAGES_A)]
+        page_b = [held([P, T2], F32, "page_b%d" % i) for i in range(PAGES_B)]
+        for page in page_a + page_b:
+            nc.vector.memset(page[:], 0.0)
+        wl_s = scale_plane(N, "wl_s")
+        ident = held([P, P], F32, "ident")
+        make_identity(nc, ident[:])
+
+        v_s = [held([P, S], U8, "v_s%d" % a) for a in range(2)]
+        v_w = [held([P, S], U32, "v_w%d" % a) for a in range(2)]
+        for a in range(2):
+            nc.vector.tensor_copy(v_w[a][:], tab_w[a][:].indirect(idx[:]))
+            nc.vector.tensor_copy(v_s[a][:], tab_s[:, a * T : (a + 1) * T].indirect(idx[:]))
+
+        def load_raw(src, a, half):
+            raw = ring.tile([P, 4, BANK], F32, name="raw", tag="raw", bufs=5)
+            rows = src[512 * a : 512 * (a + 1), BANK * half : BANK * (half + 1)]
+            nc.sync.dma_start(out=raw[:], in_=rows.rearrange("(p j) c -> p j c", j=4))
+            return raw
+
+        def interleave(raw, grouped):
+            nc.scalar.copy(
+                out=grouped[:].rearrange("p (c i) j -> p c j i", i=4),
+                in_=raw[:].rearrange("p j (c i) -> p c j i", i=4),
+            )
+
+        def quantize(codes, scales, src):
+            nc.vector.quantize_mx(out=codes.bitcast(FP8X4), scales=scales, in_=src)
+
+        wr_w, wr_s = {}, {}
+
+        def prepare_wr(half):
+            for a in range(2):
+                raw = load_raw(wr, a, half)
+                grouped = ring.tile([P, BANK, 4], BF16, name="wr_g", tag="wr_g", align_bytes=64)
+                interleave(raw, grouped)
+                wr_w[a, half] = held([P, BANK], U32, "wr_w%d%d" % (a, half))
+                wr_s[a, half] = held([P, BANK], U8, "wr_s%d%d" % (a, half))
+                quantize(wr_w[a, half][:], wr_s[a, half][:], grouped[:].rearrange("p c j -> p (c j)"))
+
+        h1, h2, fit_sb = {}, {}, {}
+
+        def donor(c):
+            acc = bank(c % 2)
+            for a in range(2):
+                mx(acc[:], wd_w[:, a, 2 * P * c : 2 * P * (c + 1)], wd_s[:, a * H + P * c : a * H + P * (c + 1)],
+                   v_w[a][:], v_s[a][:], a == 0, a == 1, FP4X4)
+            h1[c] = held([P, S], F32, "h1_%d" % c)
+            nc.scalar.activation(h1[c][:], acc[:], SILU)
+
+        def recipient(c):
+            acc = bank(2 + c % 2)
+            half, cols = c // 4, slice(P * (c % 4), P * (c % 4 + 1))
+            for a in range(2):
+                mx(acc[:], wr_w[a, half][:, cols], wr_s[a, half][:, cols], v_w[a][:], v_s[a][:], a == 0, a == 1)
+            h2[c] = held([P, S], F32, "h2_%d" % c)
+            nc.scalar.copy(out=h2[c][:], in_=acc[:])
+
+        def load_fit(c):
+            pair = ring.tile([P, 2, T2], F32, name="fit_pair", tag="raw", bufs=5)
+            nc.sync.dma_start(out=pair[:], in_=fit[P * c : P * (c + 2), :].rearrange("(h p) m -> p h m", h=2))
+            fit_sb[c], fit_sb[c + 1] = pair[:, 0, :], pair[:, 1, :]
+
+        def put_a(c):
+            nc.vector.tensor_tensor(page_a[c % PAGES_A][:].indirect(idx2[:]), h1[c][:], wg1_sb[:], MULT)
+
+        def put_b(c):
+            nc.vector.tensor_tensor(page_b[c % PAGES_B][:].indirect(idx3[:]), h2[c][:], wg2_sb[:], MULT)
+
+        zt = {}
+        work = [held([P, 2 * BANK], F32, "work%d" % b) for b in range(2)]
+
+        def meet(c):
+            a, quarter = c // 4, c % 4
+            for b in range(2):
+                cols = slice(BANK * b, BANK * (b + 1))
+                acc = bank(4 + 2 * (c % 2) + b)
+                for k in range(4):
+                    nc.tensor.matmul(acc[:, P * k : P * (k + 1)], fit_sb[c][:, BANK * b + P * k : BANK * b + P * (k + 1)],
+                                     ident[:], is_transpose=True, start=(k == 0), stop=False)
+                prod = work[b][:, BANK * (c % 2) : BANK * (c % 2 + 1)]
+                nc.vector.tensor_tensor(prod, page_a[c % PAGES_A][:, cols], page_b[c % PAGES_B][:, cols], MULT)
+                for k in range(4):
+                    nc.tensor.matmul(acc[:, P * k : P * (k + 1)], prod[:, P * k : P * (k + 1)],
+                                     ident[:], is_transpose=True, start=False, stop=(k == 3))
+                if quarter == 0:
+                    zt[a, b] = held([P, 4, 2, P, 2], BF16, "zt%d%d" % (a, b))
+                nc.scalar.copy(
+                    out=zt[a, b][:, :, :, 32 * quarter : 32 * (quarter + 1), :],
+                    in_=acc[:].rearrange("m (k q u e) -> m k u q e", k=4, u=2, e=2),
+                )
+
+        z_w, z_s = {}, {}
+
+        def turn_back(a, b):
+            words = zt[a, b][:].rearrange("m k u p e -> m (k u p e)").bitcast(F32)
+            grouped = work[b]
+            pairs = grouped[:].rearrange("p (t q u) -> p t q u", t=4, u=2)
+            for j in range(2):
+                acc = bank(6 - 2 * a + j)
+                for u in range(2):
+                    for k in range(2):
+                        blk = (2 * j + k) * 2 + u
+                        nc.tensor.transpose(acc[:, 256 * u + P * k : 256 * u + P * (k + 1)],
+                                            words[:, P * blk : P * (blk + 1)], ident[:])
+                nc.scalar.copy(out=pairs[:, :, 64 * j : 64 * (j + 1), :],
+                               in_=acc[:].rearrange("p (u q t) -> p t q u", u=2, t=4))
+            z_w[a, b] = held([P, BANK], U32, "z_w%d%d" % (a, b))
+            z_s[a, b] = held([P, BANK], U8, "z_s%d%d" % (a, b))
+            quantize(z_w[a, b][:], z_s[a, b][:], grouped[:].bitcast(BF16))
+
+        def left_pass(acc, a, b, nb):
+            ncols = slice(P * nb, P * (nb + 1))
+            for t in range(4):
+                tcols = slice(P * t, P * (t + 1))
+                mx(acc[:, tcols], z_w[a, b][:, tcols], z_s[a, b][:, tcols],
+                   wl_w[:, a, ncols], wl_s[:, a * N + P * nb : a * N + P * (nb + 1)],
+                   a == 0 and t == 0, a == 1 and t == 3)
+
+        for c in range(4):
+            donor(c)
+            if c < 2:
+                put_a(c)
+        prepare_wr(0)
+        idx3 = load_list(offs3, "idx3")
+        wg2_sb = held([P, S], F32, "wg2_sb", tag="late")
+        nc.sync.dma_start(out=wg2_sb[:], in_=wg2)
+        for c in range(4):
+            recipient(c)
+        for c in range(4, 8):
+            donor(c)
+        prepare_wr(1)
+        rm_g = {}
+        for b in range(2):
+            for half in range(2):
+                raw = load_raw(rm, b, half)
+                rm_g[b, half] = held([P, BANK, 4], BF16, "rm_g%d%d" % (b, half))
+                interleave(raw, rm_g[b, half])
+        for c in range(0, 8, 2):
+            load_fit(c)
+        wl_w = held([P, 2, N], U32, "wl_w")
+        nc.sync.dma_start(out=wl_w[:].bitcast(I32), in_=wl_words.rearrange("a p n i -> p a (n i)").bitcast(I32))
+        load_scales(nc.sync, wl_s, wl_scales)
+        gs_sb = held([P, 2, 4], F32, "gs_sb")
+        nc.sync.dma_start(out=gs_sb[:], in_=gs.rearrange("(b p t) -> p b t", b=2, t=4))
+
+        early = {}
+        for c in range(8):
+            put_b(c)
+            if c + 2 < 8:
+                put_a(c + 2)
+            meet(c)
+            if c == 1:
+                for later in range(4, 8):
+                    recipient(later)
+            if c == 4:
+                for b in range(2):
+                    turn_back(0, b)
+                for nb in range(4):
+                    early[nb] = bank(nb)
+                    left_pass(early[nb], 0, 0, nb)
+
+        for b in range(2):
+            turn_back(1, b)
+        e_g = [held([P, 2, P, 4], BF16, "e_g%d" % nb) for nb in range(4)]
+
+        def weigh(acc, b, nb):
+            nc.vector.tensor_tensor(
+                e_g[nb][:, b], acc[:].rearrange("p (t n) -> p n t", t=4),
+                gs_sb[:, b, :].unsqueeze(1).to_broadcast([P, P, 4]), MULT,
+            )
+
+        for nb in range(4):
+            left_pass(early[nb], 1, 0, nb)
+            weigh(early[nb], 0, nb)
+        rm_w = held([P, 4, BANK], U32, "rm_w", tag="late")
+        rm_s = held([P, 4, BANK], U8, "rm_s")
+        for b in range(2):
+            for half in range(2):
+                quantize(rm_w[:, 2 * b + half, :], rm_s[:, 2 * b + half, :], rm_g[b, half][:].rearrange("p c j -> p (c j)"))
+
+        def finish(nb):
+            e_w = held([P, 2 * P], U32, "e_w%d" % nb)
+            e_s = held([P, 2 * P], U8, "e_s%d" % nb)
+            quantize(e_w[:], e_s[:], e_g[nb][:].rearrange("p b n t -> p (b n t)"))
+            for half in range(2):
+                acc = bank([0, 1, 2, 3, 6, 7, 4, 5][2 * nb + half])
+                for b in range(2):
+                    bcols = slice(P * b, P * (b + 1))
+                    mx(acc[:], e_w[:, bcols], e_s[:, bcols], rm_w[:, 2 * b + half, :], rm_s[:, 2 * b + half, :], b == 0, b == 1)
+                res = held([P, BANK], F32, "res%d%d" % (nb, half), tag="h1_%d" % (2 * nb + half))
+                if nb == 3 and half == 1:
+                    nc.vector.tensor_copy(out=res[:], in_=acc[:])
+                else:
+                    nc.scalar.copy(out=res[:], in_=acc[:])
+                nc.sync.dma_start(out=out[P * nb : P * (nb + 1), BANK * half : BANK * (half + 1)], in_=res[:])
+
+        for nb in range(4):
+            acc = bank(4 + (nb + 2) % 4)
+            for a in range(2):
+                left_pass(acc, a, 1, nb)
+            weigh(acc, 1, nb)
+            if nb > 0:
+                finish(nb - 1)
+        finish(3)

@@ -16,11 +16,19 @@ FP8X4 = mybir.dt.float8_e4m3fn_x4
 FP4X4 = mybir.dt.float4_e2m1fn_x4
 MULT = mybir.AluOpType.mult
 SILU = mybir.ActivationFunctionType.Silu
+COPY = mybir.ActivationFunctionType.Copy
 
 P = 128
+PACK = 4
+K_PASS = P * PACK
 BANK = 512
+TILES = H // P
+QUARTER = T2 // 4
 PAGES_A = 3
-PAGES_B = 1
+A_AHEAD = PAGES_A - 1
+LOAD_BUFS = 6
+FINE_FROM = 6
+SCALAR_WEIGHS = (2, 3)
 
 
 def tile_list_donor_slot_mixing_kernel(
@@ -40,249 +48,319 @@ def tile_list_donor_slot_mixing_kernel(
             return psum.tile([P, BANK], F32, name="bank%d" % i, tag="bank%d" % i)
 
         def load_list(src, name):
-            t = lists.tile([P, S // 16], U16, name=name)
-            nc.sync.dma_start(t[:], src)
-            return t
+            offsets = lists.tile([P, S // 16], U16, name=name)
+            nc.sync.dma_start(offsets[:], src)
+            return offsets
 
         def scale_plane(width, name):
             plane = held([P, 2 * width], U8, name)
             nc.vector.memset(plane[:].bitcast(I32), 0)
             return plane
 
-        def load_scales(queue, plane, src):
+        def load_scales(plane, src):
             rows = src.rearrange("a (q r) c -> r q a c", r=4)
             for r in range(4):
-                queue.dma_start(
+                nc.sync.dma_start(
                     out=plane[r:P:32, :].bitcast(I32).rearrange("q (a c) -> q a c", a=2),
                     in_=rows[r].bitcast(I32),
                 )
 
-        def mx(acc, lhs, lhs_s, rhs, rhs_s, start, stop, lhs_dt=FP8X4):
+        def mx(acc, lhs, lhs_scale, rhs, rhs_scale, start, stop, lhs_dtype=FP8X4):
             nc.tensor.matmul_mx(
-                out=acc, lhsT=lhs.bitcast(lhs_dt), lhsT_scale=lhs_s, rhs=rhs.bitcast(FP8X4), rhs_scale=rhs_s,
-                start=start, stop=stop,
+                out=acc, lhsT=lhs.bitcast(lhs_dtype), lhsT_scale=lhs_scale,
+                rhs=rhs.bitcast(FP8X4), rhs_scale=rhs_scale, start=start, stop=stop,
             )
+
+        def quantize(codes, scales, src):
+            nc.vector.quantize_mx(out=codes.bitcast(FP8X4), scales=scales, in_=src)
 
         tab_s = scale_plane(T, "tab_s")
         wd_s = scale_plane(H, "wd_s")
         idx = load_list(offs, "idx")
         tab_w = [held([P, T], U32, "tab_w%d" % a) for a in range(2)]
+        wd_w = [held([P, 2, H], U8, "wd_w%d" % half) for half in range(2)]
 
         def load_tab(a):
             nc.sync.dma_start(out=tab_w[a][:].bitcast(I32), in_=tab_words[a].rearrange("p n i -> p (n i)").bitcast(I32))
 
+        def load_wd(half):
+            columns = wd_words.rearrange("a p n -> p a n")[:, :, H * half : H * (half + 1)]
+            nc.sync.dma_start(out=wd_w[half][:].bitcast(I32), in_=columns.bitcast(I32))
+
         load_tab(0)
-        load_scales(nc.sync, tab_s, tab_scales)
+        load_scales(tab_s, tab_scales)
+        load_wd(0)
         load_tab(1)
-        wd_w = held([P, 2, 2 * H], U8, "wd_w")
-        nc.sync.dma_start(out=wd_w[:].bitcast(I32), in_=wd_words.rearrange("a p n -> p a n").bitcast(I32))
-        load_scales(nc.sync, wd_s, wd_scales)
+        load_scales(wd_s, wd_scales)
         idx2 = load_list(offs2, "idx2")
         wg1_sb = held([P, S], F32, "wg1_sb")
         nc.sync.dma_start(out=wg1_sb[:], in_=wg1)
 
         page_a = [held([P, T2], F32, "page_a%d" % i) for i in range(PAGES_A)]
-        page_b = [held([P, T2], F32, "page_b%d" % i) for i in range(PAGES_B)]
+        page_b = [held([P, T2], F32, "page_b%d" % i) for i in range(2)]
         for page in page_a + page_b:
             nc.vector.memset(page[:], 0.0)
         wl_s = scale_plane(N, "wl_s")
         ident = held([P, P], F32, "ident")
         make_identity(nc, ident[:])
 
+        half_list = S // 2
         v_s = [held([P, S], U8, "v_s%d" % a) for a in range(2)]
         v_w = [held([P, S], U32, "v_w%d" % a) for a in range(2)]
+
+        def list_half(offsets, part):
+            return offsets[:, half_list // 16 * part : half_list // 16 * (part + 1)]
+
+        nc.vector.tensor_copy(v_w[0][:], tab_w[0][:].indirect(idx[:]))
         for a in range(2):
-            nc.vector.tensor_copy(v_w[a][:], tab_w[a][:].indirect(idx[:]))
             nc.vector.tensor_copy(v_s[a][:], tab_s[:, a * T : (a + 1) * T].indirect(idx[:]))
+        for part in range(2):
+            entries = slice(half_list * part, half_list * (part + 1))
+            nc.vector.tensor_copy(v_w[1][:, entries], tab_w[1][:].indirect(list_half(idx, part)))
 
-        def load_raw(src, a, half):
-            raw = ring.tile([P, 4, BANK], F32, name="raw", tag="raw", bufs=5)
-            rows = src[512 * a : 512 * (a + 1), BANK * half : BANK * (half + 1)]
-            nc.sync.dma_start(out=raw[:], in_=rows.rearrange("(p j) c -> p j c", j=4))
-            return raw
+        def load_piece(src, a, half):
+            piece = ring.tile([P, PACK, BANK], F32, name="piece", tag="stream", bufs=LOAD_BUFS)
+            rows = src[K_PASS * a : K_PASS * (a + 1), BANK * half : BANK * (half + 1)]
+            nc.sync.dma_start(out=piece[:], in_=rows.rearrange("(p i) c -> p i c", i=PACK))
+            return piece
 
-        def interleave(raw, grouped):
+        def round_and_group(piece, grouped):
             nc.scalar.copy(
-                out=grouped[:].rearrange("p (c i) j -> p c j i", i=4),
-                in_=raw[:].rearrange("p j (c i) -> p c j i", i=4),
+                out=grouped.rearrange("p (c x) i -> p c i x", x=4),
+                in_=piece[:].rearrange("p i (c x) -> p c i x", x=4),
             )
 
-        def quantize(codes, scales, src):
-            nc.vector.quantize_mx(out=codes.bitcast(FP8X4), scales=scales, in_=src)
-
-        wr_w, wr_s = {}, {}
+        wr_w, wr_s, wr_piece = {}, {}, {}
+        wr_grouped = [held([P, BANK, PACK], BF16, "wr_grouped%d" % a) for a in range(2)]
 
         def prepare_wr(half):
             for a in range(2):
-                raw = load_raw(wr, a, half)
-                grouped = ring.tile([P, BANK, 4], BF16, name="wr_g", tag="wr_g", align_bytes=64)
-                interleave(raw, grouped)
+                wr_piece[a, half] = load_piece(wr, a, half)
+                round_and_group(wr_piece[a, half], wr_grouped[a][:])
                 wr_w[a, half] = held([P, BANK], U32, "wr_w%d%d" % (a, half))
                 wr_s[a, half] = held([P, BANK], U8, "wr_s%d%d" % (a, half))
-                quantize(wr_w[a, half][:], wr_s[a, half][:], grouped[:].rearrange("p c j -> p (c j)"))
+                quantize(wr_w[a, half][:], wr_s[a, half][:], wr_grouped[a][:].rearrange("p c i -> p (c i)"))
+
+        rm_grouped = {}
+
+        def prepare_rm(n):
+            rm_grouped[n] = held([P, BANK, PACK], BF16, "rm_grouped%d" % n)
+            round_and_group(load_piece(rm, n // 2, n % 2), rm_grouped[n][:])
 
         h1, h2, fit_sb = {}, {}, {}
 
-        def donor(c):
-            acc = bank(c % 2)
-            for a in range(2):
-                mx(acc[:], wd_w[:, a, 2 * P * c : 2 * P * (c + 1)], wd_s[:, a * H + P * c : a * H + P * (c + 1)],
-                   v_w[a][:], v_s[a][:], a == 0, a == 1, FP4X4)
-            h1[c] = held([P, S], F32, "h1_%d" % c)
-            nc.scalar.activation(h1[c][:], acc[:], SILU)
+        def wd_operand(a, c):
+            words = wd_w[c // 4][:, a, 2 * P * (c % 4) : 2 * P * (c % 4 + 1)]
+            return words, wd_s[:, a * H + P * c : a * H + P * (c + 1)]
 
-        def recipient(c):
-            acc = bank(2 + c % 2)
+        def first_donor():
+            accs = [bank(part) for part in range(2)]
+            for a in range(2):
+                for part in range(2):
+                    for j in range(2):
+                        entries = slice(half_list * part + P * j, half_list * part + P * (j + 1))
+                        mx(accs[part][:, P * j : P * (j + 1)], *wd_operand(a, 0), v_w[a][:, entries], v_s[a][:, entries],
+                           a == 0 and j == 0, a == 1 and j == 1, FP4X4)
+            for part in range(2):
+                values = held([P, half_list], F32, "h1_0%d" % part)
+                nc.scalar.activation(values[:], accs[part][:, 0:half_list], SILU)
+                nc.vector.tensor_tensor(page_a[0][:].indirect(list_half(idx2, part)), values[:],
+                                        wg1_sb[:, half_list * part : half_list * (part + 1)], MULT)
+
+        def profile(name, c):
+            return held([P, S], F32, "%s_%d" % (name, c))[:]
+
+        def donor(c, acc, values):
+            for a in range(2):
+                mx(acc[:], *wd_operand(a, c), v_w[a][:], v_s[a][:], a == 0, a == 1, FP4X4)
+            h1[c] = values
+            nc.scalar.activation(values, acc[:], SILU)
+
+        def recipient(c, acc, values):
             half, cols = c // 4, slice(P * (c % 4), P * (c % 4 + 1))
             for a in range(2):
                 mx(acc[:], wr_w[a, half][:, cols], wr_s[a, half][:, cols], v_w[a][:], v_s[a][:], a == 0, a == 1)
-            h2[c] = held([P, S], F32, "h2_%d" % c)
-            nc.scalar.copy(out=h2[c][:], in_=acc[:])
+            h2[c] = values
+            nc.scalar.copy(out=values, in_=acc[:])
 
         def load_fit(c):
-            pair = ring.tile([P, 2, T2], F32, name="fit_pair", tag="raw", bufs=5)
+            pair = ring.tile([P, 2, T2], F32, name="fit_pair", tag="stream", bufs=LOAD_BUFS)
             nc.sync.dma_start(out=pair[:], in_=fit[P * c : P * (c + 2), :].rearrange("(h p) m -> p h m", h=2))
             fit_sb[c], fit_sb[c + 1] = pair[:, 0, :], pair[:, 1, :]
 
+        def page_a_of(c):
+            return page_a[c % PAGES_A]
+
+        def page_b_of(c):
+            return page_b[1 if c >= TILES - 3 else c % 2]
+
         def put_a(c):
-            nc.vector.tensor_tensor(page_a[c % PAGES_A][:].indirect(idx2[:]), h1[c][:], wg1_sb[:], MULT)
+            nc.vector.tensor_tensor(page_a_of(c)[:].indirect(idx2[:]), h1[c], wg1_sb[:], MULT)
 
         def put_b(c):
-            nc.vector.tensor_tensor(page_b[c % PAGES_B][:].indirect(idx3[:]), h2[c][:], wg2_sb[:], MULT)
+            nc.vector.tensor_tensor(page_b_of(c)[:].indirect(idx3[:]), h2[c], wg2_sb[:], MULT)
 
-        zt = {}
+        zt, sums = {}, {}
         work = [held([P, 2 * BANK], F32, "work%d" % b) for b in range(2)]
+        spare = [wr_grouped[b][:].rearrange("p c i -> p (c i)").bitcast(F32) for b in range(2)]
 
-        def meet(c):
-            a, quarter = c // 4, c % 4
-            for b in range(2):
-                cols = slice(BANK * b, BANK * (b + 1))
-                acc = bank(4 + 2 * (c % 2) + b)
-                for k in range(4):
-                    nc.tensor.matmul(acc[:, P * k : P * (k + 1)], fit_sb[c][:, BANK * b + P * k : BANK * b + P * (k + 1)],
-                                     ident[:], is_transpose=True, start=(k == 0), stop=False)
-                prod = work[b][:, BANK * (c % 2) : BANK * (c % 2 + 1)]
-                nc.vector.tensor_tensor(prod, page_a[c % PAGES_A][:, cols], page_b[c % PAGES_B][:, cols], MULT)
-                for k in range(4):
-                    nc.tensor.matmul(acc[:, P * k : P * (k + 1)], prod[:, P * k : P * (k + 1)],
-                                     ident[:], is_transpose=True, start=False, stop=(k == 3))
-                if quarter == 0:
-                    zt[a, b] = held([P, 4, 2, P, 2], BF16, "zt%d%d" % (a, b))
-                nc.scalar.copy(
-                    out=zt[a, b][:, :, :, 32 * quarter : 32 * (quarter + 1), :],
-                    in_=acc[:].rearrange("m (k q u e) -> m k u q e", k=4, u=2, e=2),
-                )
+        def open_sums(c):
+            if c < FINE_FROM:
+                sums[c] = [bank(4 + 2 * (c % 2) + b) for b in range(2)]
+            else:
+                sums[c] = [bank(4 * (c - FINE_FROM) + q) for q in range(4)]
+            width = T2 // len(sums[c])
+            for i, acc in enumerate(sums[c]):
+                for k in range(width // P):
+                    slots = slice(width * i + P * k, width * i + P * (k + 1))
+                    nc.tensor.matmul(acc[:, P * k : P * (k + 1)], fit_sb[c][:, slots], ident[:],
+                                     is_transpose=True, start=(k == 0), stop=False)
+
+        def close_sums(c):
+            a, place = c // 4, slice(32 * (c % 4), 32 * (c % 4 + 1))
+            width = T2 // len(sums[c])
+            for i, acc in enumerate(sums[c]):
+                slots = slice(width * i, width * (i + 1))
+                b, first = divmod(width * i, BANK)
+                room = spare[b] if c == 5 else work[b][:, BANK * (c % 2) : BANK * (c % 2 + 1)]
+                product = room[:, first : first + width]
+                nc.vector.tensor_tensor(product, page_a_of(c)[:, slots], page_b_of(c)[:, slots], MULT)
+                for k in range(width // P):
+                    nc.tensor.matmul(acc[:, P * k : P * (k + 1)], product[:, P * k : P * (k + 1)], ident[:],
+                                     is_transpose=True, start=False, stop=(k == width // P - 1))
+                for j in range(width // QUARTER):
+                    nc.scalar.copy(
+                        out=zt[a, width * i // QUARTER + j][:, :, :, place, :],
+                        in_=acc[:, QUARTER * j : QUARTER * (j + 1)].rearrange("m (k p u e) -> m k u p e", k=2, u=2, e=2),
+                    )
 
         z_w, z_s = {}, {}
 
-        def turn_back(a, b):
-            words = zt[a, b][:].rearrange("m k u p e -> m (k u p e)").bitcast(F32)
-            grouped = work[b]
-            pairs = grouped[:].rearrange("p (t q u) -> p t q u", t=4, u=2)
+        def turn_back(a, b, first_bank, grouped):
+            pairs = grouped.rearrange("p (t s u) -> p t s u", t=PACK, u=2)
             for j in range(2):
-                acc = bank(6 - 2 * a + j)
+                acc = bank(first_bank + j)
+                words = zt[a, 2 * b + j][:].rearrange("m k u p e -> m (k u p e)").bitcast(F32)
                 for u in range(2):
                     for k in range(2):
-                        blk = (2 * j + k) * 2 + u
-                        nc.tensor.transpose(acc[:, 256 * u + P * k : 256 * u + P * (k + 1)],
-                                            words[:, P * blk : P * (blk + 1)], ident[:])
+                        nc.tensor.transpose(acc[:, QUARTER * u + P * k : QUARTER * u + P * (k + 1)],
+                                            words[:, P * (2 * k + u) : P * (2 * k + u + 1)], ident[:])
                 nc.scalar.copy(out=pairs[:, :, 64 * j : 64 * (j + 1), :],
-                               in_=acc[:].rearrange("p (u q t) -> p t q u", u=2, t=4))
+                               in_=acc[:].rearrange("p (u s t) -> p t s u", u=2, t=PACK))
             z_w[a, b] = held([P, BANK], U32, "z_w%d%d" % (a, b))
             z_s[a, b] = held([P, BANK], U8, "z_s%d%d" % (a, b))
-            quantize(z_w[a, b][:], z_s[a, b][:], grouped[:].bitcast(BF16))
+            quantize(z_w[a, b][:], z_s[a, b][:], grouped.bitcast(BF16))
 
         def left_pass(acc, a, b, nb):
-            ncols = slice(P * nb, P * (nb + 1))
-            for t in range(4):
-                tcols = slice(P * t, P * (t + 1))
-                mx(acc[:, tcols], z_w[a, b][:, tcols], z_s[a, b][:, tcols],
-                   wl_w[:, a, ncols], wl_s[:, a * N + P * nb : a * N + P * (nb + 1)],
-                   a == 0 and t == 0, a == 1 and t == 3)
+            for t in range(PACK):
+                cols = slice(P * t, P * (t + 1))
+                mx(acc[:, cols], z_w[a, b][:, cols], z_s[a, b][:, cols],
+                   wl_w[:, a, P * nb : P * (nb + 1)], wl_s[:, a * N + P * nb : a * N + P * (nb + 1)],
+                   a == 0 and t == 0, a == 1 and t == PACK - 1)
 
-        for c in range(4):
-            donor(c)
-            if c < 2:
-                put_a(c)
+        first_donor()
+        donor(1, bank(2), profile("h1", 1))
+        put_a(1)
         prepare_wr(0)
+        load_wd(1)
+        for c in range(2, 4):
+            donor(c, bank(c % 2), wr_piece[1, 0][:, c % 2, :])
         idx3 = load_list(offs3, "idx3")
-        wg2_sb = held([P, S], F32, "wg2_sb", tag="late")
+        wg2_sb = held([P, S], F32, "wg2_sb", tag="wg2_then_rm")
         nc.sync.dma_start(out=wg2_sb[:], in_=wg2)
-        for c in range(4):
-            recipient(c)
-        for c in range(4, 8):
-            donor(c)
+        for c in range(3):
+            recipient(c, bank(2 + c % 2), profile("h2", c))
+        load_fit(0)
         prepare_wr(1)
-        rm_g = {}
-        for b in range(2):
-            for half in range(2):
-                raw = load_raw(rm, b, half)
-                rm_g[b, half] = held([P, BANK, 4], BF16, "rm_g%d%d" % (b, half))
-                interleave(raw, rm_g[b, half])
-        for c in range(0, 8, 2):
+        recipient(3, bank(3), wr_piece[1, 1][:, 0, :])
+        donor(4, bank(0), wr_piece[1, 1][:, 1, :])
+        for c in range(5, TILES):
+            donor(c, bank(c % 2), profile("h1", c))
+        for n in range(4):
+            prepare_rm(n)
+        for c in range(2, TILES, 2):
             load_fit(c)
         wl_w = held([P, 2, N], U32, "wl_w")
         nc.sync.dma_start(out=wl_w[:].bitcast(I32), in_=wl_words.rearrange("a p n i -> p a (n i)").bitcast(I32))
-        load_scales(nc.sync, wl_s, wl_scales)
-        gs_sb = held([P, 2, 4], F32, "gs_sb")
-        nc.sync.dma_start(out=gs_sb[:], in_=gs.rearrange("(b p t) -> p b t", b=2, t=4))
+        load_scales(wl_s, wl_scales)
+        gs_sb = held([P, 2, PACK], F32, "gs_sb")
+        nc.sync.dma_start(out=gs_sb[:], in_=gs.rearrange("(b s t) -> s b t", b=2, t=PACK))
 
-        early = {}
-        for c in range(8):
+        e_sum = {}
+        for c in range(TILES):
             put_b(c)
-            if c + 2 < 8:
-                put_a(c + 2)
-            meet(c)
+            if c + A_AHEAD < TILES:
+                put_a(c + A_AHEAD)
+            if c % 4 == 0:
+                for q in range(4):
+                    zt[c // 4, q] = held([P, 2, 2, P, 2], BF16, "zt%d%d" % (c // 4, q))
+            if c < TILES - 1:
+                open_sums(c)
+            close_sums(c)
             if c == 1:
-                for later in range(4, 8):
-                    recipient(later)
-            if c == 4:
+                for later in range(4, TILES):
+                    recipient(later, bank(6 + later % 2), profile("h2", later))
+            if c == 3:
                 for b in range(2):
-                    turn_back(0, b)
+                    turn_back(0, b, 6, spare[b])
+            if c == TILES - 2:
+                open_sums(TILES - 1)
                 for nb in range(4):
-                    early[nb] = bank(nb)
-                    left_pass(early[nb], 0, 0, nb)
+                    e_sum[0, nb] = bank(nb)
+                    left_pass(e_sum[0, nb], 0, 0, nb)
 
         for b in range(2):
-            turn_back(1, b)
-        e_g = [held([P, 2, P, 4], BF16, "e_g%d" % nb) for nb in range(4)]
+            turn_back(1, b, 4 + 2 * b, work[b][:])
 
-        def weigh(acc, b, nb):
-            nc.vector.tensor_tensor(
-                e_g[nb][:, b], acc[:].rearrange("p (t n) -> p n t", t=4),
-                gs_sb[:, b, :].unsqueeze(1).to_broadcast([P, P, 4]), MULT,
-            )
+        spent = work[1][:].bitcast(BF16).rearrange("s (h b n t) -> s h b n t", h=2, b=2, t=PACK)
+        e_grouped = [spent[:, 0], spent[:, 1]] + [held([P, 2, P, PACK], BF16, "e_grouped%d" % nb)[:] for nb in range(2, 4)]
 
-        for nb in range(4):
-            left_pass(early[nb], 1, 0, nb)
-            weigh(early[nb], 0, nb)
-        rm_w = held([P, 4, BANK], U32, "rm_w", tag="late")
+        def weigh(b, nb):
+            acc = e_sum[b, nb]
+            if b == 0 and nb in SCALAR_WEIGHS:
+                rows = ring.tile([P, PACK, P], BF16, name="rows", tag="rows")
+                for t in range(PACK):
+                    nc.scalar.activation(rows[:, t, :], acc[:, P * t : P * (t + 1)], COPY, scale=gs_sb[:, b, t : t + 1])
+                nc.scalar.copy(out=e_grouped[nb][:, b], in_=rows[:].rearrange("s t n -> s n t"))
+            else:
+                nc.vector.tensor_tensor(
+                    e_grouped[nb][:, b], acc[:].rearrange("s (t n) -> s n t", t=PACK),
+                    gs_sb[:, b, :].unsqueeze(1).to_broadcast([P, P, PACK]), MULT,
+                )
+
+        rm_w = held([P, 4, BANK], U32, "rm_w", tag="wg2_then_rm")
         rm_s = held([P, 4, BANK], U8, "rm_s")
-        for b in range(2):
-            for half in range(2):
-                quantize(rm_w[:, 2 * b + half, :], rm_s[:, 2 * b + half, :], rm_g[b, half][:].rearrange("p c j -> p (c j)"))
+        for n in range(4):
+            quantize(rm_w[:, n, :], rm_s[:, n, :], rm_grouped[n][:].rearrange("p c i -> p (c i)"))
 
-        def finish(nb):
-            e_w = held([P, 2 * P], U32, "e_w%d" % nb)
-            e_s = held([P, 2 * P], U8, "e_s%d" % nb)
-            quantize(e_w[:], e_s[:], e_g[nb][:].rearrange("p b n t -> p (b n t)"))
-            for half in range(2):
-                acc = bank([0, 1, 2, 3, 6, 7, 4, 5][2 * nb + half])
-                for b in range(2):
-                    bcols = slice(P * b, P * (b + 1))
-                    mx(acc[:], e_w[:, bcols], e_s[:, bcols], rm_w[:, 2 * b + half, :], rm_s[:, 2 * b + half, :], b == 0, b == 1)
-                res = held([P, BANK], F32, "res%d%d" % (nb, half), tag="h1_%d" % (2 * nb + half))
-                if nb == 3 and half == 1:
-                    nc.vector.tensor_copy(out=res[:], in_=acc[:])
-                else:
-                    nc.scalar.copy(out=res[:], in_=acc[:])
-                nc.sync.dma_start(out=out[P * nb : P * (nb + 1), BANK * half : BANK * (half + 1)], in_=res[:])
+        def open_second_half(nb):
+            e_sum[1, nb] = bank(4 + nb)
+            left_pass(e_sum[1, nb], 0, 1, nb)
+
+        for nb in range(2):
+            open_second_half(nb)
+        e_w, e_s = {}, {}
+        for nb in range(4):
+            if nb >= 2:
+                open_second_half(nb)
+            for b in range(2):
+                left_pass(e_sum[b, nb], 1, b, nb)
+            for b in range(2):
+                weigh(b, nb)
+            e_w[nb] = held([P, 2 * P], U32, "e_w%d" % nb)
+            e_s[nb] = held([P, 2 * P], U8, "e_s%d" % nb)
+            quantize(e_w[nb][:], e_s[nb][:], e_grouped[nb].rearrange("s b n t -> s (b n t)"))
 
         for nb in range(4):
-            acc = bank(4 + (nb + 2) % 4)
-            for a in range(2):
-                left_pass(acc, a, 1, nb)
-            weigh(acc, 1, nb)
-            if nb > 0:
-                finish(nb - 1)
-        finish(3)
+            for half in range(2):
+                acc = bank(nb + 4 * half)
+                for b in range(2):
+                    cols = slice(P * b, P * (b + 1))
+                    mx(acc[:], e_w[nb][:, cols], e_s[nb][:, cols], rm_w[:, 2 * b + half, :], rm_s[:, 2 * b + half, :],
+                       b == 0, b == 1)
+                result = held([P, BANK], F32, "result%d%d" % (nb, half))
+                if nb >= 2 and half == 1:
+                    nc.vector.tensor_copy(out=result[:], in_=acc[:])
+                else:
+                    nc.scalar.copy(out=result[:], in_=acc[:])
+                nc.sync.dma_start(out=out[P * nb : P * (nb + 1), BANK * half : BANK * (half + 1)], in_=result[:])

from contextlib import ExitStack

import concourse.mybir as mybir
from concourse.masks import make_identity

K, T, S, H, T2, N = 1024, 2048, 512, 1024, 1024, 512
FLOPS = 2 * (2 * K * H * S + H * T2 * N + T2 * N * T2)

F32 = mybir.dt.float32
BF16 = mybir.dt.bfloat16
I32 = mybir.dt.int32
U32 = mybir.dt.uint32
U16 = mybir.dt.uint16
U8 = mybir.dt.uint8
FP8X4 = mybir.dt.float8_e4m3fn_x4
FP4X4 = mybir.dt.float4_e2m1fn_x4
MULT = mybir.AluOpType.mult
SILU = mybir.ActivationFunctionType.Silu
COPY = mybir.ActivationFunctionType.Copy

P = 128
PACK = 4
K_PASS = P * PACK
BANK = 512
TILES = H // P
QUARTER = T2 // 4
PAGES_A = 3
A_AHEAD = PAGES_A - 1
LOAD_BUFS = 6
FINE_FROM = 6
SCALAR_WEIGHS = (2, 3)


def tile_list_donor_slot_mixing_kernel(
    tc, tab_words, tab_scales, offs, offs2, offs3, wd_words, wd_scales, wr, wg1, wg2, fit, wl_words, wl_scales, gs, rm, out
):
    nc = tc.nc
    with ExitStack() as ctx:
        lists = ctx.enter_context(tc.tile_pool(name="lists", bufs=1))
        keep = ctx.enter_context(tc.tile_pool(name="keep", bufs=1))
        ring = ctx.enter_context(tc.tile_pool(name="ring", bufs=2))
        psum = ctx.enter_context(tc.psum_pool(name="psum", bufs=1))

        def held(shape, dtype, name, tag=None):
            return keep.tile(shape, dtype, name=name, tag=tag or name, align_bytes=64)

        def bank(i):
            return psum.tile([P, BANK], F32, name="bank%d" % i, tag="bank%d" % i)

        def load_list(src, name):
            offsets = lists.tile([P, S // 16], U16, name=name)
            nc.sync.dma_start(offsets[:], src)
            return offsets

        def scale_plane(width, name):
            plane = held([P, 2 * width], U8, name)
            nc.vector.memset(plane[:].bitcast(I32), 0)
            return plane

        def load_scales(plane, src):
            rows = src.rearrange("a (q r) c -> r q a c", r=4)
            for r in range(4):
                nc.sync.dma_start(
                    out=plane[r:P:32, :].bitcast(I32).rearrange("q (a c) -> q a c", a=2),
                    in_=rows[r].bitcast(I32),
                )

        def mx(acc, lhs, lhs_scale, rhs, rhs_scale, start, stop, lhs_dtype=FP8X4):
            nc.tensor.matmul_mx(
                out=acc, lhsT=lhs.bitcast(lhs_dtype), lhsT_scale=lhs_scale,
                rhs=rhs.bitcast(FP8X4), rhs_scale=rhs_scale, start=start, stop=stop,
            )

        def quantize(codes, scales, src):
            nc.vector.quantize_mx(out=codes.bitcast(FP8X4), scales=scales, in_=src)

        tab_s = scale_plane(T, "tab_s")
        wd_s = scale_plane(H, "wd_s")
        idx = load_list(offs, "idx")
        tab_w = [held([P, T], U32, "tab_w%d" % a) for a in range(2)]
        wd_w = [held([P, 2, H], U8, "wd_w%d" % half) for half in range(2)]

        def load_tab(a):
            nc.sync.dma_start(out=tab_w[a][:].bitcast(I32), in_=tab_words[a].rearrange("p n i -> p (n i)").bitcast(I32))

        def load_wd(half):
            columns = wd_words.rearrange("a p n -> p a n")[:, :, H * half : H * (half + 1)]
            nc.sync.dma_start(out=wd_w[half][:].bitcast(I32), in_=columns.bitcast(I32))

        load_tab(0)
        load_scales(tab_s, tab_scales)
        load_wd(0)
        load_tab(1)
        load_scales(wd_s, wd_scales)
        idx2 = load_list(offs2, "idx2")
        wg1_sb = held([P, S], F32, "wg1_sb")
        nc.sync.dma_start(out=wg1_sb[:], in_=wg1)

        page_a = [held([P, T2], F32, "page_a%d" % i) for i in range(PAGES_A)]
        page_b = [held([P, T2], F32, "page_b%d" % i) for i in range(2)]
        for page in page_a + page_b:
            nc.vector.memset(page[:], 0.0)
        wl_s = scale_plane(N, "wl_s")
        ident = held([P, P], F32, "ident")
        make_identity(nc, ident[:])

        half_list = S // 2
        v_s = [held([P, S], U8, "v_s%d" % a) for a in range(2)]
        v_w = [held([P, S], U32, "v_w%d" % a) for a in range(2)]

        def list_half(offsets, part):
            return offsets[:, half_list // 16 * part : half_list // 16 * (part + 1)]

        nc.vector.tensor_copy(v_w[0][:], tab_w[0][:].indirect(idx[:]))
        for a in range(2):
            nc.vector.tensor_copy(v_s[a][:], tab_s[:, a * T : (a + 1) * T].indirect(idx[:]))
        for part in range(2):
            entries = slice(half_list * part, half_list * (part + 1))
            nc.vector.tensor_copy(v_w[1][:, entries], tab_w[1][:].indirect(list_half(idx, part)))

        def load_piece(src, a, half):
            piece = ring.tile([P, PACK, BANK], F32, name="piece", tag="stream", bufs=LOAD_BUFS)
            rows = src[K_PASS * a : K_PASS * (a + 1), BANK * half : BANK * (half + 1)]
            nc.sync.dma_start(out=piece[:], in_=rows.rearrange("(p i) c -> p i c", i=PACK))
            return piece

        def round_and_group(piece, grouped):
            nc.scalar.copy(
                out=grouped.rearrange("p (c x) i -> p c i x", x=4),
                in_=piece[:].rearrange("p i (c x) -> p c i x", x=4),
            )

        wr_w, wr_s, wr_piece = {}, {}, {}
        wr_grouped = [held([P, BANK, PACK], BF16, "wr_grouped%d" % a) for a in range(2)]

        def prepare_wr(half):
            for a in range(2):
                wr_piece[a, half] = load_piece(wr, a, half)
                round_and_group(wr_piece[a, half], wr_grouped[a][:])
                wr_w[a, half] = held([P, BANK], U32, "wr_w%d%d" % (a, half))
                wr_s[a, half] = held([P, BANK], U8, "wr_s%d%d" % (a, half))
                quantize(wr_w[a, half][:], wr_s[a, half][:], wr_grouped[a][:].rearrange("p c i -> p (c i)"))

        rm_grouped = {}

        def prepare_rm(n):
            rm_grouped[n] = held([P, BANK, PACK], BF16, "rm_grouped%d" % n)
            round_and_group(load_piece(rm, n // 2, n % 2), rm_grouped[n][:])

        h1, h2, fit_sb = {}, {}, {}

        def wd_operand(a, c):
            words = wd_w[c // 4][:, a, 2 * P * (c % 4) : 2 * P * (c % 4 + 1)]
            return words, wd_s[:, a * H + P * c : a * H + P * (c + 1)]

        def first_donor():
            accs = [bank(part) for part in range(2)]
            for a in range(2):
                for part in range(2):
                    for j in range(2):
                        entries = slice(half_list * part + P * j, half_list * part + P * (j + 1))
                        mx(accs[part][:, P * j : P * (j + 1)], *wd_operand(a, 0), v_w[a][:, entries], v_s[a][:, entries],
                           a == 0 and j == 0, a == 1 and j == 1, FP4X4)
            for part in range(2):
                values = held([P, half_list], F32, "h1_0%d" % part)
                nc.scalar.activation(values[:], accs[part][:, 0:half_list], SILU)
                nc.vector.tensor_tensor(page_a[0][:].indirect(list_half(idx2, part)), values[:],
                                        wg1_sb[:, half_list * part : half_list * (part + 1)], MULT)

        def profile(name, c):
            return held([P, S], F32, "%s_%d" % (name, c))[:]

        def donor(c, acc, values):
            for a in range(2):
                mx(acc[:], *wd_operand(a, c), v_w[a][:], v_s[a][:], a == 0, a == 1, FP4X4)
            h1[c] = values
            nc.scalar.activation(values, acc[:], SILU)

        def recipient(c, acc, values):
            half, cols = c // 4, slice(P * (c % 4), P * (c % 4 + 1))
            for a in range(2):
                mx(acc[:], wr_w[a, half][:, cols], wr_s[a, half][:, cols], v_w[a][:], v_s[a][:], a == 0, a == 1)
            h2[c] = values
            nc.scalar.copy(out=values, in_=acc[:])

        def load_fit(c):
            pair = ring.tile([P, 2, T2], F32, name="fit_pair", tag="stream", bufs=LOAD_BUFS)
            nc.sync.dma_start(out=pair[:], in_=fit[P * c : P * (c + 2), :].rearrange("(h p) m -> p h m", h=2))
            fit_sb[c], fit_sb[c + 1] = pair[:, 0, :], pair[:, 1, :]

        def page_a_of(c):
            return page_a[c % PAGES_A]

        def page_b_of(c):
            return page_b[1 if c >= TILES - 3 else c % 2]

        def put_a(c):
            nc.vector.tensor_tensor(page_a_of(c)[:].indirect(idx2[:]), h1[c], wg1_sb[:], MULT)

        def put_b(c):
            nc.vector.tensor_tensor(page_b_of(c)[:].indirect(idx3[:]), h2[c], wg2_sb[:], MULT)

        zt, sums = {}, {}
        work = [held([P, 2 * BANK], F32, "work%d" % b) for b in range(2)]
        spare = [wr_grouped[b][:].rearrange("p c i -> p (c i)").bitcast(F32) for b in range(2)]

        def open_sums(c):
            if c < FINE_FROM:
                sums[c] = [bank(4 + 2 * (c % 2) + b) for b in range(2)]
            else:
                sums[c] = [bank(4 * (c - FINE_FROM) + q) for q in range(4)]
            width = T2 // len(sums[c])
            for i, acc in enumerate(sums[c]):
                for k in range(width // P):
                    slots = slice(width * i + P * k, width * i + P * (k + 1))
                    nc.tensor.matmul(acc[:, P * k : P * (k + 1)], fit_sb[c][:, slots], ident[:],
                                     is_transpose=True, start=(k == 0), stop=False)

        def close_sums(c):
            a, place = c // 4, slice(32 * (c % 4), 32 * (c % 4 + 1))
            width = T2 // len(sums[c])
            for i, acc in enumerate(sums[c]):
                slots = slice(width * i, width * (i + 1))
                b, first = divmod(width * i, BANK)
                room = spare[b] if c == 5 else work[b][:, BANK * (c % 2) : BANK * (c % 2 + 1)]
                product = room[:, first : first + width]
                nc.vector.tensor_tensor(product, page_a_of(c)[:, slots], page_b_of(c)[:, slots], MULT)
                for k in range(width // P):
                    nc.tensor.matmul(acc[:, P * k : P * (k + 1)], product[:, P * k : P * (k + 1)], ident[:],
                                     is_transpose=True, start=False, stop=(k == width // P - 1))
                for j in range(width // QUARTER):
                    nc.scalar.copy(
                        out=zt[a, width * i // QUARTER + j][:, :, :, place, :],
                        in_=acc[:, QUARTER * j : QUARTER * (j + 1)].rearrange("m (k p u e) -> m k u p e", k=2, u=2, e=2),
                    )

        z_w, z_s = {}, {}

        def turn_back(a, b, first_bank, grouped):
            pairs = grouped.rearrange("p (t s u) -> p t s u", t=PACK, u=2)
            for j in range(2):
                acc = bank(first_bank + j)
                words = zt[a, 2 * b + j][:].rearrange("m k u p e -> m (k u p e)").bitcast(F32)
                for u in range(2):
                    for k in range(2):
                        nc.tensor.transpose(acc[:, QUARTER * u + P * k : QUARTER * u + P * (k + 1)],
                                            words[:, P * (2 * k + u) : P * (2 * k + u + 1)], ident[:])
                nc.scalar.copy(out=pairs[:, :, 64 * j : 64 * (j + 1), :],
                               in_=acc[:].rearrange("p (u s t) -> p t s u", u=2, t=PACK))
            z_w[a, b] = held([P, BANK], U32, "z_w%d%d" % (a, b))
            z_s[a, b] = held([P, BANK], U8, "z_s%d%d" % (a, b))
            quantize(z_w[a, b][:], z_s[a, b][:], grouped.bitcast(BF16))

        def left_pass(acc, a, b, nb):
            for t in range(PACK):
                cols = slice(P * t, P * (t + 1))
                mx(acc[:, cols], z_w[a, b][:, cols], z_s[a, b][:, cols],
                   wl_w[:, a, P * nb : P * (nb + 1)], wl_s[:, a * N + P * nb : a * N + P * (nb + 1)],
                   a == 0 and t == 0, a == 1 and t == PACK - 1)

        first_donor()
        donor(1, bank(2), profile("h1", 1))
        put_a(1)
        prepare_wr(0)
        load_wd(1)
        for c in range(2, 4):
            donor(c, bank(c % 2), wr_piece[1, 0][:, c % 2, :])
        idx3 = load_list(offs3, "idx3")
        wg2_sb = held([P, S], F32, "wg2_sb", tag="wg2_then_rm")
        nc.sync.dma_start(out=wg2_sb[:], in_=wg2)
        for c in range(3):
            recipient(c, bank(2 + c % 2), profile("h2", c))
        load_fit(0)
        prepare_wr(1)
        recipient(3, bank(3), wr_piece[1, 1][:, 0, :])
        donor(4, bank(0), wr_piece[1, 1][:, 1, :])
        for c in range(5, TILES):
            donor(c, bank(c % 2), profile("h1", c))
        for n in range(4):
            prepare_rm(n)
        for c in range(2, TILES, 2):
            load_fit(c)
        wl_w = held([P, 2, N], U32, "wl_w")
        nc.sync.dma_start(out=wl_w[:].bitcast(I32), in_=wl_words.rearrange("a p n i -> p a (n i)").bitcast(I32))
        load_scales(wl_s, wl_scales)
        gs_sb = held([P, 2, PACK], F32, "gs_sb")
        nc.sync.dma_start(out=gs_sb[:], in_=gs.rearrange("(b s t) -> s b t", b=2, t=PACK))

        e_sum = {}
        for c in range(TILES):
            put_b(c)
            if c + A_AHEAD < TILES:
                put_a(c + A_AHEAD)
            if c % 4 == 0:
                for q in range(4):
                    zt[c // 4, q] = held([P, 2, 2, P, 2], BF16, "zt%d%d" % (c // 4, q))
            if c < TILES - 1:
                open_sums(c)
            close_sums(c)
            if c == 1:
                for later in range(4, TILES):
                    recipient(later, bank(6 + later % 2), profile("h2", later))
            if c == 3:
                for b in range(2):
                    turn_back(0, b, 6, spare[b])
            if c == TILES - 2:
                open_sums(TILES - 1)
                for nb in range(4):
                    e_sum[0, nb] = bank(nb)
                    left_pass(e_sum[0, nb], 0, 0, nb)

        for b in range(2):
            turn_back(1, b, 4 + 2 * b, work[b][:])

        spent = work[1][:].bitcast(BF16).rearrange("s (h b n t) -> s h b n t", h=2, b=2, t=PACK)
        e_grouped = [spent[:, 0], spent[:, 1]] + [held([P, 2, P, PACK], BF16, "e_grouped%d" % nb)[:] for nb in range(2, 4)]

        def weigh(b, nb):
            acc = e_sum[b, nb]
            if b == 0 and nb in SCALAR_WEIGHS:
                rows = ring.tile([P, PACK, P], BF16, name="rows", tag="rows")
                for t in range(PACK):
                    nc.scalar.activation(rows[:, t, :], acc[:, P * t : P * (t + 1)], COPY, scale=gs_sb[:, b, t : t + 1])
                nc.scalar.copy(out=e_grouped[nb][:, b], in_=rows[:].rearrange("s t n -> s n t"))
            else:
                nc.vector.tensor_tensor(
                    e_grouped[nb][:, b], acc[:].rearrange("s (t n) -> s n t", t=PACK),
                    gs_sb[:, b, :].unsqueeze(1).to_broadcast([P, P, PACK]), MULT,
                )

        rm_w = held([P, 4, BANK], U32, "rm_w", tag="wg2_then_rm")
        rm_s = held([P, 4, BANK], U8, "rm_s")
        for n in range(4):
            quantize(rm_w[:, n, :], rm_s[:, n, :], rm_grouped[n][:].rearrange("p c i -> p (c i)"))

        def open_second_half(nb):
            e_sum[1, nb] = bank(4 + nb)
            left_pass(e_sum[1, nb], 0, 1, nb)

        for nb in range(2):
            open_second_half(nb)
        e_w, e_s = {}, {}
        for nb in range(4):
            if nb >= 2:
                open_second_half(nb)
            for b in range(2):
                left_pass(e_sum[b, nb], 1, b, nb)
            for b in range(2):
                weigh(b, nb)
            e_w[nb] = held([P, 2 * P], U32, "e_w%d" % nb)
            e_s[nb] = held([P, 2 * P], U8, "e_s%d" % nb)
            quantize(e_w[nb][:], e_s[nb][:], e_grouped[nb].rearrange("s b n t -> s (b n t)"))

        for nb in range(4):
            for half in range(2):
                acc = bank(nb + 4 * half)
                for b in range(2):
                    cols = slice(P * b, P * (b + 1))
                    mx(acc[:], e_w[nb][:, cols], e_s[nb][:, cols], rm_w[:, 2 * b + half, :], rm_s[:, 2 * b + half, :],
                       b == 0, b == 1)
                result = held([P, BANK], F32, "result%d%d" % (nb, half))
                if nb >= 2 and half == 1:
                    nc.vector.tensor_copy(out=result[:], in_=acc[:])
                else:
                    nc.scalar.copy(out=result[:], in_=acc[:])
                nc.sync.dma_start(out=out[P * nb : P * (nb + 1), BANK * half : BANK * (half + 1)], in_=result[:])
